import numpy as np
import ml_dtypes


def mxq(x, axis, fmt="e4m3"):
    dtype, down = {"e4m3": (ml_dtypes.float8_e4m3fn, 7), "e5m2": (ml_dtypes.float8_e5m2, 14)}[fmt]
    v = np.moveaxis(np.asarray(x, np.float32).astype(ml_dtypes.bfloat16).astype(np.float64), axis, -1)
    blocks = v.reshape(v.shape[:-1] + (-1, 32))
    amax = np.abs(blocks).max(-1, keepdims=True)
    byte = np.maximum(np.where(amax > 0, np.frexp(amax)[1] - 1 + 127, 0) - down, 1)
    scale = np.exp2(byte - 127.0)
    codes = (blocks / scale).astype(np.float32).astype(dtype).astype(np.float64)
    return np.moveaxis((codes * scale).reshape(v.shape), -1, axis)


WIDE = False


def mx_kscale(k):
    if not WIDE:
        return np.ones(k)
    levels = np.array([10, -10, 5, -5, 0])
    if k % 512:
        return np.exp2(np.random.permutation(np.resize(levels, k // 32))).repeat(32)
    a = np.empty((k // 512, 16))
    for p in range(k // 512):
        a[p, :8] = np.random.permutation(np.resize(levels, 8))
        for g in range(8):
            far = levels[np.abs(levels - a[p, g]) >= 10]
            a[p, g + 8] = far[np.random.randint(len(far))]
    return np.exp2(a.ravel()).repeat(32)


def f64(x):
    return np.asarray(x).astype(np.float64)


def striped(idx):
    return np.tile(np.asarray(idx).reshape(-1, 16).T, (8, 1)).astype(np.uint16)


def unstriped(offs):
    return offs[:16].T.reshape(-1).astype(np.int64)


E2M1 = np.array([0.0, 0.5, 1.0, 1.5, 2.0, 3.0, 4.0, 6.0, -0.0, -0.5, -1.0, -1.5, -2.0, -3.0, -4.0, -6.0])


def pack_weight(w, fmt):
    k, n = w.shape
    w = f64(np.asarray(w, np.float32).astype(ml_dtypes.bfloat16)).reshape(k // 32, 32, n)
    amax = np.abs(w).max(1)
    if fmt == "e4m3":
        byte = np.frexp(amax)[1] - 1 + 127 - 7
    else:
        mant, ex = np.frexp(amax / 6.0)
        byte = np.where(mant > 0.5, ex, ex - 1) + 127
    byte = np.clip(np.where(amax > 0, byte, 1), 1, 254)
    scaled = (w * np.exp2(127.0 - byte)[:, None, :]).reshape(k, n).astype(np.float32)
    by_word = np.ascontiguousarray(scaled.reshape(k // 512, 128, 4, n).transpose(0, 1, 3, 2))
    if fmt == "e4m3":
        words = by_word.astype(ml_dtypes.float8_e4m3fn).view(np.uint8)
    else:
        c = by_word.astype(ml_dtypes.float4_e2m1fn).view(np.uint8) & 0xF
        words = (c[..., 0::2] | (c[..., 1::2] << 4)).reshape(k // 512, 128, 2 * n)
    return np.ascontiguousarray(words), np.ascontiguousarray(byte.astype(np.uint8).reshape(k // 512, 16, n))


def unpack_weight(words, scales, fmt):
    g, _, n = scales.shape
    words = np.ascontiguousarray(words).reshape(g, 128, n, -1)
    if fmt == "e4m3":
        vals = words.view(ml_dtypes.float8_e4m3fn).astype(np.float64)
    else:
        nib = np.empty((g, 128, n, 4), np.uint8)
        nib[..., 0::2] = words & 0xF
        nib[..., 1::2] = words >> 4
        vals = E2M1[nib]
    vals = vals * np.repeat(np.exp2(scales.astype(np.float64) - 127.0), 8, axis=1)[..., None]
    return vals.transpose(0, 1, 3, 2).reshape(g * 512, n)


D, E, T, I, Q = 512, 512, 2048, 512, 128


def setup_inputs():
    n = np.random.standard_normal
    idx = np.random.permutation(T)[:I]
    fd = mx_kscale(D)
    fe = mx_kscale(E)
    keysp = pack_weight(n((D, T)) / fd[:, None], "e4m3")
    valsp = pack_weight(n((E, T)) / fe[:, None], "e4m3")
    return {
        "query": (n((D, Q)) * 0.6 / np.sqrt(D) * fd[:, None]).astype(np.float32),
        "keys_words": keysp[0],
        "keys_scales": keysp[1],
        "age": np.tile(np.random.uniform(0.0, 2.0, T), (128, 1)).astype(np.float32),
        "rate": (np.random.uniform(0.3, 1.2, (Q, 1))).astype(np.float32),
        "reserve": (np.random.uniform(20.0, 100.0, (Q, 1))).astype(np.float32),
        "gout": (n((E, Q)) * 1 / np.sqrt(E) * fe[:, None]).astype(np.float32),
        "vals_words": valsp[0],
        "vals_scales": valsp[1],
        "size": (np.random.uniform(0.5, 2.0, (1, I))).astype(np.float32),
        "old": (0.5 * n((Q, T))).astype(np.float32),
        "offs": striped(idx),
    }


def reference(query, keys_words, keys_scales, age, rate, reserve, gout, vals_words, vals_scales, size, old, offs):
    idx = unstriped(offs)
    keysu = unpack_weight(keys_words, keys_scales, "e4m3")
    valsu = unpack_weight(vals_words, vals_scales, "e4m3")
    queryq = mxq(f64(query), 0, "e4m3")
    keysidxg = keysu[:, idx]
    a = queryq.T @ keysidxg
    p = np.exp(a - f64(age)[:1][:, idx] * f64(rate))
    z = np.sum(p, axis=1, keepdims=True) + f64(reserve)
    goutq = mxq(f64(gout), 0, "e4m3")
    valsidxg = valsu[:, idx]
    c0 = goutq.T @ valsidxg
    dz = np.sum(c0 * p * f64(size) / np.square(z) * (-1.0), axis=1, keepdims=True)
    dp = c0 / z * f64(size) + dz
    da = dp * p
    gs = da * 512.0
    gf = np.zeros((Q, T))
    gf[:, idx] = gs
    y = f64(old) + gf
    return y

@@ -1,0 +1,153 @@
+from contextlib import ExitStack
+
+import concourse.mybir as mybir
+from concourse.masks import make_identity
+
+D, E, T, I, Q = 512, 512, 2048, 512, 128
+FLOPS = 2 * (D + E) * Q * I
+BYTES = 4 * (D * Q + E * Q + T + 2 * Q + I + 2 * Q * T) + (D + E) * T + (D + E) // 32 * T + 2 * 128 * (I // 16)
+
+F32 = mybir.dt.float32
+BF16 = mybir.dt.bfloat16
+I32 = mybir.dt.int32
+U32 = mybir.dt.uint32
+U16 = mybir.dt.uint16
+U8 = mybir.dt.uint8
+FP8X4 = mybir.dt.float8_e4m3fn_x4
+ALU = mybir.AluOpType
+ACT = mybir.ActivationFunctionType
+
+P = 128
+PACK = 4
+BANK = 512
+OUT_CHUNKS = (512, 512, 512, 512)
+
+
+def tile_attend_bfadereserve_s_kernel(tc, query, keys_words, keys_scales, age, rate, reserve, gout, vals_words, vals_scales, size, old, offs, out):
+    nc = tc.nc
+    with ExitStack() as ctx:
+        sb = ctx.enter_context(tc.tile_pool(name="sb", bufs=1))
+        shared = ctx.enter_context(tc.tile_pool(name="shared", bufs=1))
+        ps = ctx.enter_context(tc.psum_pool(name="ps", bufs=1))
+
+        offsets = sb.tile([P, I // 16], U16, name="offsets")
+        nc.sync.dma_start(offsets[:], offs)
+
+        def load_scales(queue, scales, name):
+            plane = sb.tile([P, T], U8, name=name)
+            nc.vector.memset(plane[:].bitcast(I32), 0)
+            for quad in range(4):
+                queue.dma_start(plane[32 * quad : 32 * quad + 4, :].bitcast(I32), scales[0, 4 * quad : 4 * quad + 4, :].bitcast(I32))
+            return plane
+
+        def load_words(words, pool_words):
+            nc.sync.dma_start(pool_words[:].bitcast(I32), words[0].rearrange("p n t -> p (n t)").bitcast(I32))
+            return pool_words
+
+        def load_rows(x, raw):
+            nc.sync.dma_start(raw[:], x.rearrange("(p j) w -> p j w", j=PACK))
+            return raw
+
+        def interleave(raw, name):
+            grouped = sb.tile([P, Q, PACK], BF16, name=name, align_bytes=64)
+            nc.scalar.copy(grouped[:], raw[:].rearrange("p j w -> p w j"))
+            return grouped
+
+        def quantize(grouped, name):
+            codes = sb.tile([P, Q], U32, name=name + "_codes", align_bytes=64)
+            scales = sb.tile([P, Q], U8, name=name + "_scales", align_bytes=64)
+            nc.vector.quantize_mx(out=codes[:].bitcast(FP8X4), scales=scales[:], in_=grouped[:].rearrange("p w j -> p (w j)"))
+            return codes, scales
+
+        def gather(window, dtype, name):
+            picked = sb.tile([P, I], dtype, name=name, align_bytes=64)
+            nc.vector.tensor_copy(picked[:], window[:].indirect(offsets[:]))
+            return picked
+
+        age_cols = sb.tile([P, T // P], F32, name="age_cols")
+        nc.sync.dma_start(age_cols[:], age[0, :].rearrange("(n j) -> n j", n=P))
+        q_raw = load_rows(query, shared.tile([P, PACK, Q], F32, name="q_raw", offset=4 * T - 1024))
+        k_words = load_words(keys_words, sb.tile([P, T], U32, name="k_words"))
+        k_plane = load_scales(nc.scalar, keys_scales, "k_plane")
+
+        ident = sb.tile([P, P], F32, name="ident")
+        make_identity(nc, ident[:])
+        v_plane = load_scales(nc.gpsimd, vals_scales, "v_plane")
+        placed = sb.tile([P, T], F32, name="placed")
+        nc.vector.memset(placed[:], 0.0)
+
+        k_sc = gather(k_plane, U8, "k_sc")
+        q_bf = interleave(q_raw, "q_bf")
+        rate_sb = shared.tile([P, 1], F32, name="rate_sb", offset=4 * T)
+        nc.sync.dma_start(rate_sb[:], rate)
+        g_raw = load_rows(gout, shared.tile([P, PACK, Q], F32, name="g_raw", offset=4 * T + 96))
+        v_words = load_words(vals_words, shared.tile([P, T], U32, name="v_words", offset=0))
+        size_cols = shared.tile([P, I // P], F32, name="size_cols", offset=4 * T + 32)
+        nc.sync.dma_start(size_cols[:], size[0, :].rearrange("(n j) -> n j", n=P))
+        reserve_sb = shared.tile([P, 1], F32, name="reserve_sb", offset=4 * T + 64)
+        nc.sync.dma_start(reserve_sb[:], reserve)
+        q_codes, q_scales = quantize(q_bf, "q")
+
+        def spread(cols, first, name):
+            bank = ps.tile([P, PACK, P], F32, name=name)
+            for j in range(PACK):
+                nc.tensor.transpose(bank[:, j, :], cols[:, first + j : first + j + 1].to_broadcast([P, P]), ident[:])
+            return bank
+
+        age_all = sb.tile([P, T], F32, name="age_all")
+        age_view = age_all[:].rearrange("p (n b j) -> p b n j", b=4, j=PACK)
+        for b in range(4):
+            bank = spread(age_cols, PACK * b, "age_bank%d" % b)
+            nc.scalar.copy(age_view[:, b], bank[:].rearrange("p j n -> p n j"))
+
+        k_g = gather(k_words, U32, "k_g")
+        a_ps = ps.tile([P, I], F32, name="a_ps")
+        nc.tensor.matmul_mx(out=a_ps[:], lhsT=q_codes[:].bitcast(FP8X4), lhsT_scale=q_scales[:], rhs=k_g[:].bitcast(FP8X4), rhs_scale=k_sc[:], start=True, stop=True)
+        age_g = gather(age_all, F32, "age_g")
+        size_bank = spread(size_cols, 0, "size_bank")
+
+        neg_s = sb.tile([P, I], F32, name="neg_s")
+        nc.vector.scalar_tensor_tensor(neg_s[:], age_g[:], rate_sb[:], a_ps[:], ALU.mult, ALU.subtract)
+        neg_m = sb.tile([P, 1], F32, name="neg_m")
+        spare = sb.tile([P, I], F32, name="spare")
+        nc.vector.tensor_scalar(spare[:], neg_s[:], 1.0, 0.0, ALU.mult, ALU.min, accum_out=neg_m[:])
+        p = sb.tile([P, I], F32, name="p")
+        p_sum = sb.tile([P, 1], F32, name="p_sum")
+        nc.scalar.activation(p[:], neg_s[:], ACT.Exp, bias=neg_m[:], scale=-1.0, accum_out=p_sum[:])
+        shrink = sb.tile([P, 1], F32, name="shrink")
+        nc.scalar.activation(shrink[:], neg_m[:], ACT.Exp)
+        neg_reserve = sb.tile([P, 1], F32, name="neg_reserve")
+        nc.scalar.mul(neg_reserve[:], reserve_sb[:], -1.0)
+
+        g_bf = interleave(g_raw, "g_bf")
+        old_sb = shared.tile([P, T], F32, name="old_sb", offset=4 * T + 96)
+        nc.sync.dma_start(old_sb[:], old)
+        g_codes, g_scales = quantize(g_bf, "g")
+        v_sc = gather(v_plane, U8, "v_sc")
+        v_g = gather(v_words, U32, "v_g")
+        c_ps = ps.tile([P, I], F32, name="c_ps")
+        nc.tensor.matmul_mx(out=c_ps[:], lhsT=g_codes[:].bitcast(FP8X4), lhsT_scale=g_scales[:], rhs=v_g[:].bitcast(FP8X4), rhs_scale=v_sc[:], start=True, stop=True)
+
+        neg_z = sb.tile([P, 1], F32, name="neg_z")
+        nc.vector.tensor_scalar(neg_z[:], shrink[:], neg_reserve[:], p_sum[:], ALU.mult, ALU.subtract)
+        p_size = sb.tile([P, I], F32, name="p_size")
+        nc.vector.tensor_tensor(p_size[:].rearrange("p (n j) -> p n j", j=PACK), p[:].rearrange("p (n j) -> p n j", j=PACK), size_bank[:].rearrange("p j n -> p n j"), ALU.mult)
+        neg_rz = sb.tile([P, 1], F32, name="neg_rz")
+        nc.vector.reciprocal(neg_rz[:], neg_z[:])
+        alpha = sb.tile([P, 1], F32, name="alpha")
+        nc.scalar.mul(alpha[:], neg_rz[:], -512.0)
+
+        direct = sb.tile([P, I], F32, name="direct")
+        d_sum = sb.tile([P, 1], F32, name="d_sum")
+        nc.vector.scalar_tensor_tensor(direct[:], c_ps[:], 1.0, p_size[:], ALU.mult, ALU.mult, accum_out=d_sum[:])
+        via_z = sb.tile([P, I], F32, name="via_z")
+        nc.vector.tensor_scalar(via_z[:], p[:], d_sum[:], neg_rz[:], ALU.mult, ALU.mult)
+        nc.vector.tensor_tensor(placed[:].indirect(offsets[:]), direct[:], via_z[:], ALU.add)
+
+        result = sb.tile([P, T], F32, name="result")
+        lo = 0
+        for width in OUT_CHUNKS:
+            cols = slice(lo, lo + width)
+            nc.vector.scalar_tensor_tensor(result[:, cols], placed[:, cols], alpha[:], old_sb[:, cols], ALU.mult, ALU.add)
+            nc.sync.dma_start(out[:, cols], result[:, cols])
+            lo += width

@@ -1,3 +1,4 @@
+import math
 from contextlib import ExitStack
 
 import concourse.mybir as mybir
@@ -20,7 +21,8 @@ ACT = mybir.ActivationFunctionType
 P = 128
 PACK = 4
 BANK = 512
-OUT_CHUNKS = (512, 512, 512, 512)
+SOFTEN = 8.0
+OUT_CHUNKS = (256, 512, 512, 512, 256)
 
 
 def tile_attend_bfadereserve_s_kernel(tc, query, keys_words, keys_scales, age, rate, reserve, gout, vals_words, vals_scales, size, old, offs, out):
@@ -28,39 +30,37 @@ def tile_attend_bfadereserve_s_kernel(tc, query, keys_words, keys_scales, age, r
     with ExitStack() as ctx:
         sb = ctx.enter_context(tc.tile_pool(name="sb", bufs=1))
         shared = ctx.enter_context(tc.tile_pool(name="shared", bufs=1))
+        arena = ctx.enter_context(tc.tile_pool(name="arena", bufs=1))
         ps = ctx.enter_context(tc.psum_pool(name="ps", bufs=1))
 
         offsets = sb.tile([P, I // 16], U16, name="offsets")
         nc.sync.dma_start(offsets[:], offs)
 
-        def load_scales(queue, scales, name):
-            plane = sb.tile([P, T], U8, name=name)
+        def load_scales(queue, scales, plane):
             nc.vector.memset(plane[:].bitcast(I32), 0)
             for quad in range(4):
                 queue.dma_start(plane[32 * quad : 32 * quad + 4, :].bitcast(I32), scales[0, 4 * quad : 4 * quad + 4, :].bitcast(I32))
             return plane
 
         def load_words(words, pool_words):
-            nc.sync.dma_start(pool_words[:].bitcast(I32), words[0].rearrange("p n t -> p (n t)").bitcast(I32))
+            nc.scalar.dma_start(pool_words[:].bitcast(I32), words[0].rearrange("p n t -> p (n t)").bitcast(I32))
             return pool_words
 
         def load_rows(x, raw):
-            nc.sync.dma_start(raw[:], x.rearrange("(p j) w -> p j w", j=PACK))
+            nc.scalar.dma_start(raw[:], x.rearrange("(p j) w -> p j w", j=PACK))
             return raw
 
-        def interleave(raw, name):
-            grouped = sb.tile([P, Q, PACK], BF16, name=name, align_bytes=64)
+        def interleave(raw, grouped):
             nc.scalar.copy(grouped[:], raw[:].rearrange("p j w -> p w j"))
             return grouped
 
-        def quantize(grouped, name):
-            codes = sb.tile([P, Q], U32, name=name + "_codes", align_bytes=64)
+        def quantize(grouped, name, tag):
+            codes = sb.tile([P, Q], U32, name=name + "_codes", tag=tag, align_bytes=64)
             scales = sb.tile([P, Q], U8, name=name + "_scales", align_bytes=64)
             nc.vector.quantize_mx(out=codes[:].bitcast(FP8X4), scales=scales[:], in_=grouped[:].rearrange("p w j -> p (w j)"))
             return codes, scales
 
-        def gather(window, dtype, name):
-            picked = sb.tile([P, I], dtype, name=name, align_bytes=64)
+        def gather(window, picked):
             nc.vector.tensor_copy(picked[:], window[:].indirect(offsets[:]))
             return picked
 
@@ -68,63 +68,66 @@ def tile_attend_bfadereserve_s_kernel(tc, query, keys_words, keys_scales, age, r
         nc.sync.dma_start(age_cols[:], age[0, :].rearrange("(n j) -> n j", n=P))
         q_raw = load_rows(query, shared.tile([P, PACK, Q], F32, name="q_raw", offset=4 * T - 1024))
         k_words = load_words(keys_words, sb.tile([P, T], U32, name="k_words"))
-        k_plane = load_scales(nc.scalar, keys_scales, "k_plane")
+        k_plane = load_scales(nc.sync, keys_scales, sb.tile([P, T], U8, name="k_plane"))
 
         ident = sb.tile([P, P], F32, name="ident")
         make_identity(nc, ident[:])
-        v_plane = load_scales(nc.gpsimd, vals_scales, "v_plane")
         placed = sb.tile([P, T], F32, name="placed")
         nc.vector.memset(placed[:], 0.0)
 
-        k_sc = gather(k_plane, U8, "k_sc")
-        q_bf = interleave(q_raw, "q_bf")
+        q_bf = interleave(q_raw, arena.tile([P, Q, PACK], BF16, name="q_bf", offset=512, align_bytes=64))
         rate_sb = shared.tile([P, 1], F32, name="rate_sb", offset=4 * T)
         nc.sync.dma_start(rate_sb[:], rate)
         g_raw = load_rows(gout, shared.tile([P, PACK, Q], F32, name="g_raw", offset=4 * T + 96))
         v_words = load_words(vals_words, shared.tile([P, T], U32, name="v_words", offset=0))
         size_cols = shared.tile([P, I // P], F32, name="size_cols", offset=4 * T + 32)
-        nc.sync.dma_start(size_cols[:], size[0, :].rearrange("(n j) -> n j", n=P))
+        nc.gpsimd.dma_start(size_cols[:], size[0, :].rearrange("(n j) -> n j", n=P))
         reserve_sb = shared.tile([P, 1], F32, name="reserve_sb", offset=4 * T + 64)
-        nc.sync.dma_start(reserve_sb[:], reserve)
-        q_codes, q_scales = quantize(q_bf, "q")
+        nc.gpsimd.dma_start(reserve_sb[:], reserve)
+        q_codes, q_scales = quantize(q_bf, "q", "q_codes")
+        v_plane = load_scales(nc.sync, vals_scales, arena.tile([P, T], U8, name="v_plane", offset=1024, align_bytes=64))
+        k_sc = gather(k_plane, arena.tile([P, I], U8, name="k_sc", offset=256, align_bytes=64))
 
-        def spread(cols, first, name):
-            bank = ps.tile([P, PACK, P], F32, name=name)
+        def spread(cols, first, name, tag):
+            bank = ps.tile([P, PACK, P], F32, name=name, tag=tag)
             for j in range(PACK):
                 nc.tensor.transpose(bank[:, j, :], cols[:, first + j : first + j + 1].to_broadcast([P, P]), ident[:])
             return bank
 
-        age_all = sb.tile([P, T], F32, name="age_all")
+        age_all = sb.tile([P, T], F32, name="age_all", tag="age_all", align_bytes=64)
         age_view = age_all[:].rearrange("p (n b j) -> p b n j", b=4, j=PACK)
         for b in range(4):
-            bank = spread(age_cols, PACK * b, "age_bank%d" % b)
+            bank = spread(age_cols, PACK * b, "age_bank%d" % b, "age_bank%d" % b)
             nc.scalar.copy(age_view[:, b], bank[:].rearrange("p j n -> p n j"))
 
-        k_g = gather(k_words, U32, "k_g")
-        a_ps = ps.tile([P, I], F32, name="a_ps")
+        k_g = gather(k_words, sb.tile([P, I], U32, name="k_g", align_bytes=64))
+        a_ps = ps.tile([P, I], F32, name="a_ps", tag="age_bank3")
         nc.tensor.matmul_mx(out=a_ps[:], lhsT=q_codes[:].bitcast(FP8X4), lhsT_scale=q_scales[:], rhs=k_g[:].bitcast(FP8X4), rhs_scale=k_sc[:], start=True, stop=True)
-        age_g = gather(age_all, F32, "age_g")
-        size_bank = spread(size_cols, 0, "size_bank")
+        age_g = gather(age_all, sb.tile([P, I], F32, name="age_g", tag="age_g", align_bytes=64))
 
-        neg_s = sb.tile([P, I], F32, name="neg_s")
-        nc.vector.scalar_tensor_tensor(neg_s[:], age_g[:], rate_sb[:], a_ps[:], ALU.mult, ALU.subtract)
+        neg_s = sb.tile([P, I + 1], F32, name="neg_s")
+        nc.gpsimd.memset(neg_s[:, I : I + 1], 0.0)
+        nc.vector.scalar_tensor_tensor(neg_s[:, :I], age_g[:], rate_sb[:], a_ps[:], ALU.mult, ALU.subtract)
+        size_bank = spread(size_cols, 0, "size_bank", "age_bank3")
         neg_m = sb.tile([P, 1], F32, name="neg_m")
-        spare = sb.tile([P, I], F32, name="spare")
-        nc.vector.tensor_scalar(spare[:], neg_s[:], 1.0, 0.0, ALU.mult, ALU.min, accum_out=neg_m[:])
+        soft = sb.tile([P, I + 1], F32, name="soft")
+        soft_sum = sb.tile([P, 1], F32, name="soft_sum")
+        nc.scalar.activation(soft[:], neg_s[:], ACT.Exp, scale=-1.0 / SOFTEN, accum_out=soft_sum[:])
+        nc.scalar.activation(neg_m[:], soft_sum[:].bitcast(U32), ACT.Copy, scale=-SOFTEN * math.log(2.0) / 2**23, bias=SOFTEN * math.log(2.0) * 127)
         p = sb.tile([P, I], F32, name="p")
         p_sum = sb.tile([P, 1], F32, name="p_sum")
-        nc.scalar.activation(p[:], neg_s[:], ACT.Exp, bias=neg_m[:], scale=-1.0, accum_out=p_sum[:])
+        nc.scalar.activation(p[:], neg_s[:, :I], ACT.Exp, bias=neg_m[:], scale=-1.0, accum_out=p_sum[:])
         shrink = sb.tile([P, 1], F32, name="shrink")
         nc.scalar.activation(shrink[:], neg_m[:], ACT.Exp)
         neg_reserve = sb.tile([P, 1], F32, name="neg_reserve")
         nc.scalar.mul(neg_reserve[:], reserve_sb[:], -1.0)
 
-        g_bf = interleave(g_raw, "g_bf")
+        g_bf = interleave(g_raw, sb.tile([P, Q, PACK], BF16, name="g_bf", tag="age_all", align_bytes=64))
         old_sb = shared.tile([P, T], F32, name="old_sb", offset=4 * T + 96)
-        nc.sync.dma_start(old_sb[:], old)
-        g_codes, g_scales = quantize(g_bf, "g")
-        v_sc = gather(v_plane, U8, "v_sc")
-        v_g = gather(v_words, U32, "v_g")
+        nc.scalar.dma_start(old_sb[:], old)
+        g_codes, g_scales = quantize(g_bf, "g", "g_codes")
+        v_sc = gather(v_plane, sb.tile([P, I], U8, name="v_sc", tag="age_g", align_bytes=64))
+        v_g = gather(v_words, arena.tile([P, I], U32, name="v_g", offset=2048, align_bytes=64))
         c_ps = ps.tile([P, I], F32, name="c_ps")
         nc.tensor.matmul_mx(out=c_ps[:], lhsT=g_codes[:].bitcast(FP8X4), lhsT_scale=g_scales[:], rhs=v_g[:].bitcast(FP8X4), rhs_scale=v_sc[:], start=True, stop=True)
 

@@ -2,7 +2,6 @@ import math
 from contextlib import ExitStack
 
 import concourse.mybir as mybir
-from concourse.masks import make_identity
 
 D, E, T, I, Q = 512, 512, 2048, 512, 128
 FLOPS = 2 * (D + E) * Q * I
@@ -20,42 +19,54 @@ ACT = mybir.ActivationFunctionType
 
 P = 128
 PACK = 4
-BANK = 512
+AGE_BANKS = T // (PACK * P)
+GRAD_SCALE = 512.0
 SOFTEN = 8.0
 OUT_CHUNKS = (256, 512, 512, 512, 256)
+
+K_WORDS_AT = 0
+Q_BF_AT = K_WORDS_AT + 4 * T
+V_PLANE_AT = Q_BF_AT + 2 * PACK * Q
+PLACED_AT = V_PLANE_AT + T
+RAMP_AT = Q_BF_AT - 64
+RAMP_WORDS = (PLACED_AT + 64 - RAMP_AT) // 4
+
+V_WORDS_AT = 0
+RATE_AT = V_WORDS_AT + 4 * T
+SIZE_AT = RATE_AT + 32
+RESERVE_AT = SIZE_AT + 32
+G_RAW_AT = RESERVE_AT + 32
+Q_RAW_AT = RATE_AT - 2 * PACK * Q
 
 
 def tile_attend_bfadereserve_s_kernel(tc, query, keys_words, keys_scales, age, rate, reserve, gout, vals_words, vals_scales, size, old, offs, out):
     nc = tc.nc
     with ExitStack() as ctx:
         sb = ctx.enter_context(tc.tile_pool(name="sb", bufs=1))
-        shared = ctx.enter_context(tc.tile_pool(name="shared", bufs=1))
-        arena = ctx.enter_context(tc.tile_pool(name="arena", bufs=1))
+        late = ctx.enter_context(tc.tile_pool(name="late", bufs=1))
+        early = ctx.enter_context(tc.tile_pool(name="early", bufs=1))
         ps = ctx.enter_context(tc.psum_pool(name="ps", bufs=1))
 
-        offsets = sb.tile([P, I // 16], U16, name="offsets")
-        nc.sync.dma_start(offsets[:], offs)
-
-        def load_scales(queue, scales, plane):
+        def load_plane(scales, plane):
             nc.vector.memset(plane[:].bitcast(I32), 0)
             for quad in range(4):
-                queue.dma_start(plane[32 * quad : 32 * quad + 4, :].bitcast(I32), scales[0, 4 * quad : 4 * quad + 4, :].bitcast(I32))
+                nc.sync.dma_start(plane[32 * quad : 32 * quad + 4, :].bitcast(I32), scales[0, 4 * quad : 4 * quad + 4, :].bitcast(I32))
             return plane
 
-        def load_words(words, pool_words):
-            nc.scalar.dma_start(pool_words[:].bitcast(I32), words[0].rearrange("p n t -> p (n t)").bitcast(I32))
-            return pool_words
+        def load_words(words, window):
+            nc.sync.dma_start(window[:].bitcast(I32), words[0].rearrange("p n t -> p (n t)").bitcast(I32))
+            return window
 
-        def load_rows(x, raw):
-            nc.scalar.dma_start(raw[:], x.rearrange("(p j) w -> p j w", j=PACK))
+        def load_rows(queue, x, raw):
+            queue.dma_start(raw[:], x.rearrange("(p j) w -> p j w", j=PACK))
             return raw
 
-        def interleave(raw, grouped):
-            nc.scalar.copy(grouped[:], raw[:].rearrange("p j w -> p w j"))
+        def interleave(copy, raw, grouped):
+            copy(grouped[:], raw[:].rearrange("p j w -> p w j"))
             return grouped
 
-        def quantize(grouped, name, tag):
-            codes = sb.tile([P, Q], U32, name=name + "_codes", tag=tag, align_bytes=64)
+        def quantize(grouped, name):
+            codes = sb.tile([P, Q], U32, name=name + "_codes", align_bytes=64)
             scales = sb.tile([P, Q], U8, name=name + "_scales", align_bytes=64)
             nc.vector.quantize_mx(out=codes[:].bitcast(FP8X4), scales=scales[:], in_=grouped[:].rearrange("p w j -> p (w j)"))
             return codes, scales
@@ -64,51 +75,60 @@ def tile_attend_bfadereserve_s_kernel(tc, query, keys_words, keys_scales, age, r
             nc.vector.tensor_copy(picked[:], window[:].indirect(offsets[:]))
             return picked
 
-        age_cols = sb.tile([P, T // P], F32, name="age_cols")
-        nc.sync.dma_start(age_cols[:], age[0, :].rearrange("(n j) -> n j", n=P))
-        q_raw = load_rows(query, shared.tile([P, PACK, Q], F32, name="q_raw", offset=4 * T - 1024))
-        k_words = load_words(keys_words, sb.tile([P, T], U32, name="k_words"))
-        k_plane = load_scales(nc.sync, keys_scales, sb.tile([P, T], U8, name="k_plane"))
-
-        ident = sb.tile([P, P], F32, name="ident")
-        make_identity(nc, ident[:])
-        placed = sb.tile([P, T], F32, name="placed")
-        nc.vector.memset(placed[:], 0.0)
-
-        q_bf = interleave(q_raw, arena.tile([P, Q, PACK], BF16, name="q_bf", offset=512, align_bytes=64))
-        rate_sb = shared.tile([P, 1], F32, name="rate_sb", offset=4 * T)
-        nc.sync.dma_start(rate_sb[:], rate)
-        g_raw = load_rows(gout, shared.tile([P, PACK, Q], F32, name="g_raw", offset=4 * T + 96))
-        v_words = load_words(vals_words, shared.tile([P, T], U32, name="v_words", offset=0))
-        size_cols = shared.tile([P, I // P], F32, name="size_cols", offset=4 * T + 32)
-        nc.gpsimd.dma_start(size_cols[:], size[0, :].rearrange("(n j) -> n j", n=P))
-        reserve_sb = shared.tile([P, 1], F32, name="reserve_sb", offset=4 * T + 64)
-        nc.gpsimd.dma_start(reserve_sb[:], reserve)
-        q_codes, q_scales = quantize(q_bf, "q", "q_codes")
-        v_plane = load_scales(nc.sync, vals_scales, arena.tile([P, T], U8, name="v_plane", offset=1024, align_bytes=64))
-        k_sc = gather(k_plane, arena.tile([P, I], U8, name="k_sc", offset=256, align_bytes=64))
-
         def spread(cols, first, name, tag):
             bank = ps.tile([P, PACK, P], F32, name=name, tag=tag)
             for j in range(PACK):
                 nc.tensor.transpose(bank[:, j, :], cols[:, first + j : first + j + 1].to_broadcast([P, P]), ident[:])
             return bank
 
-        age_all = sb.tile([P, T], F32, name="age_all", tag="age_all", align_bytes=64)
-        age_view = age_all[:].rearrange("p (n b j) -> p b n j", b=4, j=PACK)
-        for b in range(4):
-            bank = spread(age_cols, PACK * b, "age_bank%d" % b, "age_bank%d" % b)
-            nc.scalar.copy(age_view[:, b], bank[:].rearrange("p j n -> p n j"))
+        def product(acc, codes, scales, words, plane):
+            nc.tensor.matmul_mx(out=acc[:], lhsT=codes[:].bitcast(FP8X4), lhsT_scale=scales[:], rhs=words[:].bitcast(FP8X4), rhs_scale=plane[:], start=True, stop=True)
+            return acc
 
-        k_g = gather(k_words, sb.tile([P, I], U32, name="k_g", align_bytes=64))
-        a_ps = ps.tile([P, I], F32, name="a_ps", tag="age_bank3")
-        nc.tensor.matmul_mx(out=a_ps[:], lhsT=q_codes[:].bitcast(FP8X4), lhsT_scale=q_scales[:], rhs=k_g[:].bitcast(FP8X4), rhs_scale=k_sc[:], start=True, stop=True)
-        age_g = gather(age_all, sb.tile([P, I], F32, name="age_g", tag="age_g", align_bytes=64))
+        offsets = sb.tile([P, I // 16], U16, name="offsets")
+        nc.sync.dma_start(offsets[:], offs)
+        age_cols = sb.tile([P, T // P], F32, name="age_cols")
+        nc.sync.dma_start(age_cols[:], age[0, :].rearrange("(n j) -> n j", n=P))
+        q_raw = load_rows(nc.scalar, query, late.tile([P, PACK, Q], F32, name="q_raw", offset=Q_RAW_AT))
+        k_plane = load_plane(keys_scales, sb.tile([P, T], U8, name="k_plane"))
+
+        ramp = early.tile([P, RAMP_WORDS], I32, name="ramp", offset=RAMP_AT)
+        nc.gpsimd.iota(ramp[:, :P], [[1, P]], base=0, channel_multiplier=-1)
+        ident = sb.tile([P, P], F32, name="ident")
+        nc.vector.tensor_scalar(ident[:], ramp[:, :P], 0.0, None, ALU.is_equal)
+        k_words = load_words(keys_words, early.tile([P, T], U32, name="k_words", offset=K_WORDS_AT))
+        v_plane = load_plane(vals_scales, early.tile([P, T], U8, name="v_plane", offset=V_PLANE_AT))
+        placed = early.tile([P, T], F32, name="placed", offset=PLACED_AT)
+        nc.vector.memset(placed[:], 0.0)
+
+        q_bf = interleave(nc.vector.tensor_copy, q_raw, early.tile([P, Q, PACK], BF16, name="q_bf", offset=Q_BF_AT, align_bytes=64))
+        rate_sb = late.tile([P, 1], F32, name="rate_sb", offset=RATE_AT)
+        nc.sync.dma_start(rate_sb[:], rate)
+        g_raw = load_rows(nc.sync, gout, late.tile([P, PACK, Q], F32, name="g_raw", offset=G_RAW_AT))
+        v_words = load_words(vals_words, late.tile([P, T], U32, name="v_words", offset=V_WORDS_AT))
+        size_cols = late.tile([P, I // P], F32, name="size_cols", offset=SIZE_AT)
+        nc.gpsimd.dma_start(size_cols[:], size[0, :].rearrange("(n j) -> n j", n=P))
+        reserve_sb = late.tile([P, 1], F32, name="reserve_sb", offset=RESERVE_AT)
+        nc.gpsimd.dma_start(reserve_sb[:], reserve)
+        q_codes, q_scales = quantize(q_bf, "q")
+        k_scales_g = gather(k_plane, early.tile([P, I], U8, name="k_scales_g", offset=Q_BF_AT, align_bytes=64))
+
+        age_all = sb.tile([P, T], F32, name="age_all", tag="age_all", align_bytes=64)
+        age_view = age_all[:].rearrange("p (n b j) -> p b n j", b=AGE_BANKS, j=PACK)
+        for b in range(AGE_BANKS):
+            bank = spread(age_cols, PACK * b, "age_bank%d" % b, "bank%d" % b)
+            nc.scalar.copy(age_view[:, b], bank[:].rearrange("p j n -> p n j"))
+        last_bank = "bank%d" % (AGE_BANKS - 1)
+
+        k_words_g = gather(k_words, sb.tile([P, I], U32, name="k_words_g", align_bytes=64))
+        scores = product(ps.tile([P, I], F32, name="scores", tag=last_bank), q_codes, q_scales, k_words_g, k_scales_g)
+        age_g = gather(age_all, early.tile([P, I], F32, name="age_g", offset=K_WORDS_AT))
 
         neg_s = sb.tile([P, I + 1], F32, name="neg_s")
         nc.gpsimd.memset(neg_s[:, I : I + 1], 0.0)
-        nc.vector.scalar_tensor_tensor(neg_s[:, :I], age_g[:], rate_sb[:], a_ps[:], ALU.mult, ALU.subtract)
-        size_bank = spread(size_cols, 0, "size_bank", "age_bank3")
+        nc.vector.scalar_tensor_tensor(neg_s[:, :I], age_g[:], rate_sb[:], scores[:], ALU.mult, ALU.subtract)
+        size_bank = spread(size_cols, 0, "size_bank", last_bank)
+
         neg_m = sb.tile([P, 1], F32, name="neg_m")
         soft = sb.tile([P, I + 1], F32, name="soft")
         soft_sum = sb.tile([P, 1], F32, name="soft_sum")
@@ -122,35 +142,34 @@ def tile_attend_bfadereserve_s_kernel(tc, query, keys_words, keys_scales, age, r
         neg_reserve = sb.tile([P, 1], F32, name="neg_reserve")
         nc.scalar.mul(neg_reserve[:], reserve_sb[:], -1.0)
 
-        g_bf = interleave(g_raw, sb.tile([P, Q, PACK], BF16, name="g_bf", tag="age_all", align_bytes=64))
-        old_sb = shared.tile([P, T], F32, name="old_sb", offset=4 * T + 96)
-        nc.scalar.dma_start(old_sb[:], old)
-        g_codes, g_scales = quantize(g_bf, "g", "g_codes")
-        v_sc = gather(v_plane, sb.tile([P, I], U8, name="v_sc", tag="age_g", align_bytes=64))
-        v_g = gather(v_words, arena.tile([P, I], U32, name="v_g", offset=2048, align_bytes=64))
-        c_ps = ps.tile([P, I], F32, name="c_ps")
-        nc.tensor.matmul_mx(out=c_ps[:], lhsT=g_codes[:].bitcast(FP8X4), lhsT_scale=g_scales[:], rhs=v_g[:].bitcast(FP8X4), rhs_scale=v_sc[:], start=True, stop=True)
+        g_bf = interleave(nc.scalar.copy, g_raw, sb.tile([P, Q, PACK], BF16, name="g_bf", tag="age_all", align_bytes=64))
+        old_sb = late.tile([P, T], F32, name="old_sb", offset=G_RAW_AT)
+        nc.sync.dma_start(old_sb[:], old)
+        g_codes, g_scales = quantize(g_bf, "g")
+        v_scales_g = gather(v_plane, early.tile([P, I], U8, name="v_scales_g", offset=K_WORDS_AT, align_bytes=64))
+        v_words_g = gather(v_words, early.tile([P, I], U32, name="v_words_g", offset=V_PLANE_AT, align_bytes=64))
+        c = product(ps.tile([P, I], F32, name="c"), g_codes, g_scales, v_words_g, v_scales_g)
 
-        neg_z = sb.tile([P, 1], F32, name="neg_z")
+        neg_z = late.tile([P, 1], F32, name="neg_z", offset=V_WORDS_AT + 4 * I)
         nc.vector.tensor_scalar(neg_z[:], shrink[:], neg_reserve[:], p_sum[:], ALU.mult, ALU.subtract)
-        p_size = sb.tile([P, I], F32, name="p_size")
+        p_size = late.tile([P, I], F32, name="p_size", offset=V_WORDS_AT)
         nc.vector.tensor_tensor(p_size[:].rearrange("p (n j) -> p n j", j=PACK), p[:].rearrange("p (n j) -> p n j", j=PACK), size_bank[:].rearrange("p j n -> p n j"), ALU.mult)
         neg_rz = sb.tile([P, 1], F32, name="neg_rz")
         nc.vector.reciprocal(neg_rz[:], neg_z[:])
-        alpha = sb.tile([P, 1], F32, name="alpha")
-        nc.scalar.mul(alpha[:], neg_rz[:], -512.0)
+        row_factor = sb.tile([P, 1], F32, name="row_factor")
+        nc.scalar.mul(row_factor[:], neg_rz[:], -GRAD_SCALE)
 
         direct = sb.tile([P, I], F32, name="direct")
-        d_sum = sb.tile([P, 1], F32, name="d_sum")
-        nc.vector.scalar_tensor_tensor(direct[:], c_ps[:], 1.0, p_size[:], ALU.mult, ALU.mult, accum_out=d_sum[:])
+        direct_sum = sb.tile([P, 1], F32, name="direct_sum")
+        nc.vector.scalar_tensor_tensor(direct[:], c[:], 1.0, p_size[:], ALU.mult, ALU.mult, accum_out=direct_sum[:])
         via_z = sb.tile([P, I], F32, name="via_z")
-        nc.vector.tensor_scalar(via_z[:], p[:], d_sum[:], neg_rz[:], ALU.mult, ALU.mult)
+        nc.vector.tensor_scalar(via_z[:], p[:], direct_sum[:], neg_rz[:], ALU.mult, ALU.mult)
         nc.vector.tensor_tensor(placed[:].indirect(offsets[:]), direct[:], via_z[:], ALU.add)
 
         result = sb.tile([P, T], F32, name="result")
         lo = 0
         for width in OUT_CHUNKS:
             cols = slice(lo, lo + width)
-            nc.vector.scalar_tensor_tensor(result[:, cols], placed[:, cols], alpha[:], old_sb[:, cols], ALU.mult, ALU.add)
+            nc.vector.scalar_tensor_tensor(result[:, cols], placed[:, cols], row_factor[:], old_sb[:, cols], ALU.mult, ALU.add)
             nc.sync.dma_start(out[:, cols], result[:, cols])
             lo += width

@@ -133,7 +133,7 @@ def tile_attend_bfadereserve_s_kernel(tc, query, keys_words, keys_scales, age, r
         soft = sb.tile([P, I + 1], F32, name="soft")
         soft_sum = sb.tile([P, 1], F32, name="soft_sum")
         nc.scalar.activation(soft[:], neg_s[:], ACT.Exp, scale=-1.0 / SOFTEN, accum_out=soft_sum[:])
-        nc.scalar.activation(neg_m[:], soft_sum[:].bitcast(U32), ACT.Copy, scale=-SOFTEN * math.log(2.0) / 2**23, bias=SOFTEN * math.log(2.0) * 127)
+        nc.scalar.activation(neg_m[:], soft_sum[:].bitcast(U32), ACT.Copy, scale=-SOFTEN * math.log(2.0) / 2**23, bias=SOFTEN * (127 * math.log(2.0) + math.log(I + 1) / 2))
         p = sb.tile([P, I], F32, name="p")
         p_sum = sb.tile([P, 1], F32, name="p_sum")
         nc.scalar.activation(p[:], neg_s[:, :I], ACT.Exp, bias=neg_m[:], scale=-1.0, accum_out=p_sum[:])
@@ -163,7 +163,7 @@ def tile_attend_bfadereserve_s_kernel(tc, query, keys_words, keys_scales, age, r
         direct_sum = sb.tile([P, 1], F32, name="direct_sum")
         nc.vector.scalar_tensor_tensor(direct[:], c[:], 1.0, p_size[:], ALU.mult, ALU.mult, accum_out=direct_sum[:])
         via_z = sb.tile([P, I], F32, name="via_z")
-        nc.vector.tensor_scalar(via_z[:], p[:], direct_sum[:], neg_rz[:], ALU.mult, ALU.mult)
+        nc.vector.tensor_scalar(via_z[:], p[:], neg_rz[:], direct_sum[:], ALU.mult, ALU.mult)
         nc.vector.tensor_tensor(placed[:].indirect(offsets[:]), direct[:], via_z[:], ALU.add)
 
         result = sb.tile([P, T], F32, name="result")

import math
from contextlib import ExitStack

import concourse.mybir as mybir

D, E, T, I, Q = 512, 512, 2048, 512, 128
FLOPS = 2 * (D + E) * Q * I
BYTES = 4 * (D * Q + E * Q + T + 2 * Q + I + 2 * Q * T) + (D + E) * T + (D + E) // 32 * T + 2 * 128 * (I // 16)

F32 = mybir.dt.float32
BF16 = mybir.dt.bfloat16
I32 = mybir.dt.int32
U32 = mybir.dt.uint32
U16 = mybir.dt.uint16
U8 = mybir.dt.uint8
FP8X4 = mybir.dt.float8_e4m3fn_x4
ALU = mybir.AluOpType
ACT = mybir.ActivationFunctionType

P = 128
PACK = 4
AGE_BANKS = T // (PACK * P)
GRAD_SCALE = 512.0
SOFTEN = 8.0
OUT_CHUNKS = (256, 512, 512, 512, 256)

K_WORDS_AT = 0
Q_BF_AT = K_WORDS_AT + 4 * T
V_PLANE_AT = Q_BF_AT + 2 * PACK * Q
PLACED_AT = V_PLANE_AT + T
RAMP_AT = Q_BF_AT - 64
RAMP_WORDS = (PLACED_AT + 64 - RAMP_AT) // 4

V_WORDS_AT = 0
RATE_AT = V_WORDS_AT + 4 * T
SIZE_AT = RATE_AT + 32
RESERVE_AT = SIZE_AT + 32
G_RAW_AT = RESERVE_AT + 32
Q_RAW_AT = RATE_AT - 2 * PACK * Q


def tile_attend_bfadereserve_s_kernel(tc, query, keys_words, keys_scales, age, rate, reserve, gout, vals_words, vals_scales, size, old, offs, out):
    nc = tc.nc
    with ExitStack() as ctx:
        sb = ctx.enter_context(tc.tile_pool(name="sb", bufs=1))
        late = ctx.enter_context(tc.tile_pool(name="late", bufs=1))
        early = ctx.enter_context(tc.tile_pool(name="early", bufs=1))
        ps = ctx.enter_context(tc.psum_pool(name="ps", bufs=1))

        def load_plane(scales, plane):
            nc.vector.memset(plane[:].bitcast(I32), 0)
            for quad in range(4):
                nc.sync.dma_start(plane[32 * quad : 32 * quad + 4, :].bitcast(I32), scales[0, 4 * quad : 4 * quad + 4, :].bitcast(I32))
            return plane

        def load_words(words, window):
            nc.sync.dma_start(window[:].bitcast(I32), words[0].rearrange("p n t -> p (n t)").bitcast(I32))
            return window

        def load_rows(queue, x, raw):
            queue.dma_start(raw[:], x.rearrange("(p j) w -> p j w", j=PACK))
            return raw

        def interleave(copy, raw, grouped):
            copy(grouped[:], raw[:].rearrange("p j w -> p w j"))
            return grouped

        def quantize(grouped, name):
            codes = sb.tile([P, Q], U32, name=name + "_codes", align_bytes=64)
            scales = sb.tile([P, Q], U8, name=name + "_scales", align_bytes=64)
            nc.vector.quantize_mx(out=codes[:].bitcast(FP8X4), scales=scales[:], in_=grouped[:].rearrange("p w j -> p (w j)"))
            return codes, scales

        def gather(window, picked):
            nc.vector.tensor_copy(picked[:], window[:].indirect(offsets[:]))
            return picked

        def spread(cols, first, name, tag):
            bank = ps.tile([P, PACK, P], F32, name=name, tag=tag)
            for j in range(PACK):
                nc.tensor.transpose(bank[:, j, :], cols[:, first + j : first + j + 1].to_broadcast([P, P]), ident[:])
            return bank

        def product(acc, codes, scales, words, plane):
            nc.tensor.matmul_mx(out=acc[:], lhsT=codes[:].bitcast(FP8X4), lhsT_scale=scales[:], rhs=words[:].bitcast(FP8X4), rhs_scale=plane[:], start=True, stop=True)
            return acc

        offsets = sb.tile([P, I // 16], U16, name="offsets")
        nc.sync.dma_start(offsets[:], offs)
        age_cols = sb.tile([P, T // P], F32, name="age_cols")
        nc.sync.dma_start(age_cols[:], age[0, :].rearrange("(n j) -> n j", n=P))
        q_raw = load_rows(nc.scalar, query, late.tile([P, PACK, Q], F32, name="q_raw", offset=Q_RAW_AT))
        k_plane = load_plane(keys_scales, sb.tile([P, T], U8, name="k_plane"))

        ramp = early.tile([P, RAMP_WORDS], I32, name="ramp", offset=RAMP_AT)
        nc.gpsimd.iota(ramp[:, :P], [[1, P]], base=0, channel_multiplier=-1)
        ident = sb.tile([P, P], F32, name="ident")
        nc.vector.tensor_scalar(ident[:], ramp[:, :P], 0.0, None, ALU.is_equal)
        k_words = load_words(keys_words, early.tile([P, T], U32, name="k_words", offset=K_WORDS_AT))
        v_plane = load_plane(vals_scales, early.tile([P, T], U8, name="v_plane", offset=V_PLANE_AT))
        placed = early.tile([P, T], F32, name="placed", offset=PLACED_AT)
        nc.vector.memset(placed[:], 0.0)

        q_bf = interleave(nc.vector.tensor_copy, q_raw, early.tile([P, Q, PACK], BF16, name="q_bf", offset=Q_BF_AT, align_bytes=64))
        rate_sb = late.tile([P, 1], F32, name="rate_sb", offset=RATE_AT)
        nc.sync.dma_start(rate_sb[:], rate)
        g_raw = load_rows(nc.sync, gout, late.tile([P, PACK, Q], F32, name="g_raw", offset=G_RAW_AT))
        v_words = load_words(vals_words, late.tile([P, T], U32, name="v_words", offset=V_WORDS_AT))
        size_cols = late.tile([P, I // P], F32, name="size_cols", offset=SIZE_AT)
        nc.gpsimd.dma_start(size_cols[:], size[0, :].rearrange("(n j) -> n j", n=P))
        reserve_sb = late.tile([P, 1], F32, name="reserve_sb", offset=RESERVE_AT)
        nc.gpsimd.dma_start(reserve_sb[:], reserve)
        q_codes, q_scales = quantize(q_bf, "q")
        k_scales_g = gather(k_plane, early.tile([P, I], U8, name="k_scales_g", offset=Q_BF_AT, align_bytes=64))

        age_all = sb.tile([P, T], F32, name="age_all", tag="age_all", align_bytes=64)
        age_view = age_all[:].rearrange("p (n b j) -> p b n j", b=AGE_BANKS, j=PACK)
        for b in range(AGE_BANKS):
            bank = spread(age_cols, PACK * b, "age_bank%d" % b, "bank%d" % b)
            nc.scalar.copy(age_view[:, b], bank[:].rearrange("p j n -> p n j"))
        last_bank = "bank%d" % (AGE_BANKS - 1)

        k_words_g = gather(k_words, sb.tile([P, I], U32, name="k_words_g", align_bytes=64))
        scores = product(ps.tile([P, I], F32, name="scores", tag=last_bank), q_codes, q_scales, k_words_g, k_scales_g)
        age_g = gather(age_all, early.tile([P, I], F32, name="age_g", offset=K_WORDS_AT))

        neg_s = sb.tile([P, I + 1], F32, name="neg_s")
        nc.gpsimd.memset(neg_s[:, I : I + 1], 0.0)
        nc.vector.scalar_tensor_tensor(neg_s[:, :I], age_g[:], rate_sb[:], scores[:], ALU.mult, ALU.subtract)
        size_bank = spread(size_cols, 0, "size_bank", last_bank)

        neg_m = sb.tile([P, 1], F32, name="neg_m")
        soft = sb.tile([P, I + 1], F32, name="soft")
        soft_sum = sb.tile([P, 1], F32, name="soft_sum")
        nc.scalar.activation(soft[:], neg_s[:], ACT.Exp, scale=-1.0 / SOFTEN, accum_out=soft_sum[:])
        nc.scalar.activation(neg_m[:], soft_sum[:].bitcast(U32), ACT.Copy, scale=-SOFTEN * math.log(2.0) / 2**23, bias=SOFTEN * (127 * math.log(2.0) + math.log(I + 1) / 2))
        p = sb.tile([P, I], F32, name="p")
        p_sum = sb.tile([P, 1], F32, name="p_sum")
        nc.scalar.activation(p[:], neg_s[:, :I], ACT.Exp, bias=neg_m[:], scale=-1.0, accum_out=p_sum[:])
        shrink = sb.tile([P, 1], F32, name="shrink")
        nc.scalar.activation(shrink[:], neg_m[:], ACT.Exp)
        neg_reserve = sb.tile([P, 1], F32, name="neg_reserve")
        nc.scalar.mul(neg_reserve[:], reserve_sb[:], -1.0)

        g_bf = interleave(nc.scalar.copy, g_raw, sb.tile([P, Q, PACK], BF16, name="g_bf", tag="age_all", align_bytes=64))
        old_sb = late.tile([P, T], F32, name="old_sb", offset=G_RAW_AT)
        nc.sync.dma_start(old_sb[:], old)
        g_codes, g_scales = quantize(g_bf, "g")
        v_scales_g = gather(v_plane, early.tile([P, I], U8, name="v_scales_g", offset=K_WORDS_AT, align_bytes=64))
        v_words_g = gather(v_words, early.tile([P, I], U32, name="v_words_g", offset=V_PLANE_AT, align_bytes=64))
        c = product(ps.tile([P, I], F32, name="c"), g_codes, g_scales, v_words_g, v_scales_g)

        neg_z = late.tile([P, 1], F32, name="neg_z", offset=V_WORDS_AT + 4 * I)
        nc.vector.tensor_scalar(neg_z[:], shrink[:], neg_reserve[:], p_sum[:], ALU.mult, ALU.subtract)
        p_size = late.tile([P, I], F32, name="p_size", offset=V_WORDS_AT)
        nc.vector.tensor_tensor(p_size[:].rearrange("p (n j) -> p n j", j=PACK), p[:].rearrange("p (n j) -> p n j", j=PACK), size_bank[:].rearrange("p j n -> p n j"), ALU.mult)
        neg_rz = sb.tile([P, 1], F32, name="neg_rz")
        nc.vector.reciprocal(neg_rz[:], neg_z[:])
        row_factor = sb.tile([P, 1], F32, name="row_factor")
        nc.scalar.mul(row_factor[:], neg_rz[:], -GRAD_SCALE)

        direct = sb.tile([P, I], F32, name="direct")
        direct_sum = sb.tile([P, 1], F32, name="direct_sum")
        nc.vector.scalar_tensor_tensor(direct[:], c[:], 1.0, p_size[:], ALU.mult, ALU.mult, accum_out=direct_sum[:])
        via_z = sb.tile([P, I], F32, name="via_z")
        nc.vector.tensor_scalar(via_z[:], p[:], neg_rz[:], direct_sum[:], ALU.mult, ALU.mult)
        nc.vector.tensor_tensor(placed[:].indirect(offsets[:]), direct[:], via_z[:], ALU.add)

        result = sb.tile([P, T], F32, name="result")
        lo = 0
        for width in OUT_CHUNKS:
            cols = slice(lo, lo + width)
            nc.vector.scalar_tensor_tensor(result[:, cols], placed[:, cols], row_factor[:], old_sb[:, cols], ALU.mult, ALU.add)
            nc.sync.dma_start(out[:, cols], result[:, cols])
            lo += width
